import numpy as np
import ml_dtypes


def mxq(x, axis, fmt="e4m3"):
    dtype, down = {"e4m3": (ml_dtypes.float8_e4m3fn, 7), "e5m2": (ml_dtypes.float8_e5m2, 14)}[fmt]
    v = np.moveaxis(np.asarray(x, np.float32).astype(ml_dtypes.bfloat16).astype(np.float64), axis, -1)
    blocks = v.reshape(v.shape[:-1] + (-1, 32))
    amax = np.abs(blocks).max(-1, keepdims=True)
    byte = np.maximum(np.where(amax > 0, np.frexp(amax)[1] - 1 + 127, 0) - down, 1)
    scale = np.exp2(byte - 127.0)
    codes = (blocks / scale).astype(np.float32).astype(dtype).astype(np.float64)
    return np.moveaxis((codes * scale).reshape(v.shape), -1, axis)


WIDE = False


def mx_kscale(k):
    if not WIDE:
        return np.ones(k)
    levels = np.array([30, -30])
    if k % 512:
        return np.exp2(np.random.permutation(np.resize(levels, k // 32))).repeat(32)
    a = np.empty((k // 512, 16))
    for p in range(k // 512):
        a[p, :8] = np.random.permutation(np.resize(levels, 8))
        for g in range(8):
            far = levels[np.abs(levels - a[p, g]) >= 10]
            a[p, g + 8] = far[np.random.randint(len(far))]
    return np.exp2(a.ravel()).repeat(32)


def f64(x):
    return np.asarray(x).astype(np.float64)


def striped(idx):
    return np.tile(np.asarray(idx).reshape(-1, 16).T, (8, 1)).astype(np.uint16)


def unstriped(offs):
    return offs[:16].T.reshape(-1).astype(np.int64)


E2M1 = np.array([0.0, 0.5, 1.0, 1.5, 2.0, 3.0, 4.0, 6.0, -0.0, -0.5, -1.0, -1.5, -2.0, -3.0, -4.0, -6.0])


def pack_weight(w, fmt):
    k, n = w.shape
    w = f64(np.asarray(w, np.float32).astype(ml_dtypes.bfloat16)).reshape(k // 32, 32, n)
    amax = np.abs(w).max(1)
    if fmt in ("e4m3", "e5m2"):
        byte = np.frexp(amax)[1] - 1 + 127 - (7 if fmt == "e4m3" else 14)
    else:
        mant, ex = np.frexp(amax / 6.0)
        byte = np.where(mant > 0.5, ex, ex - 1) + 127
    byte = np.clip(np.where(amax > 0, byte, 1), 1, 254)
    scaled = (w * np.exp2(127.0 - byte)[:, None, :]).reshape(k, n).astype(np.float32)
    by_word = np.ascontiguousarray(scaled.reshape(k // 512, 128, 4, n).transpose(0, 1, 3, 2))
    if fmt in ("e4m3", "e5m2"):
        words = by_word.astype(ml_dtypes.float8_e4m3fn if fmt == "e4m3" else ml_dtypes.float8_e5m2).view(np.uint8)
    else:
        c = by_word.astype(ml_dtypes.float4_e2m1fn).view(np.uint8) & 0xF
        words = (c[..., 0::2] | (c[..., 1::2] << 4)).reshape(k // 512, 128, 2 * n)
    return np.ascontiguousarray(words), np.ascontiguousarray(byte.astype(np.uint8).reshape(k // 512, 16, n))


def unpack_weight(words, scales, fmt):
    g, _, n = scales.shape
    words = np.ascontiguousarray(words).reshape(g, 128, n, -1)
    if fmt in ("e4m3", "e5m2"):
        vals = words.view(ml_dtypes.float8_e4m3fn if fmt == "e4m3" else ml_dtypes.float8_e5m2).astype(np.float64)
    else:
        nib = np.empty((g, 128, n, 4), np.uint8)
        nib[..., 0::2] = words & 0xF
        nib[..., 1::2] = words >> 4
        vals = E2M1[nib]
    vals = vals * np.repeat(np.exp2(scales.astype(np.float64) - 127.0), 8, axis=1)[..., None]
    return vals.transpose(0, 1, 3, 2).reshape(g * 512, n)


def sigmoid(v):
    return 1.0 / (1.0 + np.exp(-v))


def sgn(shape):
    return np.random.uniform(0.5, 2.0, shape) * np.where(np.random.standard_normal(shape) < 0, -1.0, 1.0)


K, T, J, R, F, Z, C, O, N, L, E = 512, 1024, 256, 512, 512, 1024, 512, 128, 256, 512, 1024


def setup_inputs():
    n = np.random.standard_normal
    idx = np.random.permutation(T)[:J]
    idx2 = np.random.permutation(Z)[:J]
    idx3 = np.random.permutation(C)[:J]
    idx4 = np.random.permutation(C)[:O]
    idx5 = np.random.permutation(C)[:O]
    idx6 = np.random.permutation(J)[:O]
    idx7 = np.random.permutation(E)[:O]
    ff = mx_kscale(F)
    fk = mx_kscale(K)
    fr = mx_kscale(R)
    fl = mx_kscale(L)
    xop = pack_weight(n((F, Z)) / ff[:, None], "e2m1")
    wp = pack_weight(n((K, R)) * 1 / np.sqrt(K) / fk[:, None], "e2m1")
    w2p = pack_weight(n((F, R)) * 1 / np.sqrt(F) * ff[:, None], "e5m2")
    wbp = pack_weight(n((R, N)) * 1 / np.sqrt(R) / fr[:, None], "e5m2")
    sxp = pack_weight(n((L, O)) / fl[:, None], "e2m1")
    wsp = pack_weight(n((L, N)) * 1 / np.sqrt(L) * fl[:, None], "e5m2")
    return {
        "xo_words": xop[0],
        "xo_scales": xop[1],
        "cq": (np.random.randint(-7, 8, (K, T)).astype(np.float64)).astype(np.float32),
        "gs": (np.random.uniform(0.1, 0.4, (K, 1)) * fk[:, None]).astype(np.float32),
        "w_words": wp[0],
        "w_scales": wp[1],
        "w2_words": w2p[0],
        "w2_scales": w2p[1],
        "sa": (np.random.uniform(0.5, 1.6, (R, 1)) * fr[:, None]).astype(np.float32),
        "sb": (np.random.uniform(0.5, 1.6, (R, 1)) * fr[:, None]).astype(np.float32),
        "sg": (sgn((R, 1))).astype(np.float32),
        "bg": (np.random.uniform(-2.0, 2.0, (R, 1))).astype(np.float32),
        "wb_words": wbp[0],
        "wb_scales": wbp[1],
        "sx_words": sxp[0],
        "sx_scales": sxp[1],
        "ws_words": wsp[0],
        "ws_scales": wsp[1],
        "offs": striped(idx),
        "offs2": striped(idx2),
        "offs3": striped(idx3),
        "offs4": striped(idx4),
        "offs5": striped(idx5),
        "offs6": striped(idx6),
        "offs7": striped(idx7),
    }


def reference(xo_words, xo_scales, cq, gs, w_words, w_scales, w2_words, w2_scales, sa, sb, sg, bg, wb_words, wb_scales, sx_words, sx_scales, ws_words, ws_scales, offs, offs2, offs3, offs4, offs5, offs6, offs7):
    idx = unstriped(offs)
    idx2 = unstriped(offs2)
    idx3 = unstriped(offs3)
    idx4 = unstriped(offs4)
    idx5 = unstriped(offs5)
    idx6 = unstriped(offs6)
    idx7 = unstriped(offs7)
    xou = unpack_weight(xo_words, xo_scales, "e2m1")
    wu = unpack_weight(w_words, w_scales, "e2m1")
    w2u = unpack_weight(w2_words, w2_scales, "e5m2")
    wbu = unpack_weight(wb_words, wb_scales, "e5m2")
    sxu = unpack_weight(sx_words, sx_scales, "e2m1")
    wsu = unpack_weight(ws_words, ws_scales, "e5m2")
    x1 = f64(cq)[:, idx] * f64(gs)
    x1q = mxq(x1, 0, "e4m3")
    a = wu.T @ x1q
    xoidx2g = xou[:, idx2]
    b = w2u.T @ xoidx2g
    pw = np.zeros((R, C))
    pw[:, idx3] = a
    hid = pw[:, idx4] * f64(sa) * sigmoid(pw[:, idx5] * f64(sg) + f64(bg)) - b[:, idx6] * f64(sb)
    hidq = mxq(hid, 0, "e4m3")
    p = wbu.T @ hidq + wsu.T @ sxu
    y = np.zeros((N, E))
    y[:, idx7] = p
    return y

@@ -1,0 +1,211 @@
+from contextlib import ExitStack
+
+import concourse.mybir as mybir
+
+K, T, J, R, F, Z, C, O, N, L, E = 512, 1024, 256, 512, 512, 1024, 512, 128, 256, 512, 1024
+FLOPS = 2 * (K * R * J + F * R * J + R * N * O + L * N * O)
+
+F32 = mybir.dt.float32
+BF16 = mybir.dt.bfloat16
+I32 = mybir.dt.int32
+U32 = mybir.dt.uint32
+U16 = mybir.dt.uint16
+U8 = mybir.dt.uint8
+E4M3 = mybir.dt.float8_e4m3fn_x4
+E5M2 = mybir.dt.float8_e5m2_x4
+E2M1 = mybir.dt.float4_e2m1fn_x4
+ACT = mybir.ActivationFunctionType
+ALU = mybir.AluOpType
+
+P = 128
+PACK = 4
+QUADS = 4
+ROWS = 4
+
+
+def tile_list_gatedreadless_codednote_further_scattered_kernel(
+    tc, xo_words, xo_scales, cq, gs, w_words, w_scales, w2_words, w2_scales, sa, sb, sg, bg,
+    wb_words, wb_scales, sx_words, sx_scales, ws_words, ws_scales,
+    offs, offs2, offs3, offs4, offs5, offs6, offs7, out,
+):
+    nc = tc.nc
+    with ExitStack() as ctx:
+        keep = ctx.enter_context(tc.tile_pool(name="keep", bufs=1))
+        psum = ctx.enter_context(tc.psum_pool(name="psum", bufs=1))
+
+        def sbuf(name, shape, dtype):
+            return keep.tile(shape, dtype, name=name, align_bytes=64)
+
+        def load_list(name, src):
+            dst = sbuf(name, list(src.shape), U16)
+            nc.sync.dma_start(dst[:], src)
+            return dst
+
+        def load_by_slot(queue, name, src):
+            dst = sbuf(name, [P, PACK], F32)
+            queue.dma_start(dst[:], src.rearrange("(p t) o -> p (t o)", t=PACK))
+            return dst
+
+        def load_words(name, src, columns, dtype):
+            dst = sbuf(name, [P, columns], dtype)
+            nc.sync.dma_start(dst[:].bitcast(I32), src.bitcast(I32))
+            return dst
+
+        def stage_scales(dst, src):
+            nc.scalar.dma_start(dst, src[0].rearrange("(q r) n -> r q n", r=ROWS).bitcast(I32))
+
+        def spread_scales(plane, staged):
+            for q in range(QUADS):
+                nc.vector.tensor_copy(plane[:].bitcast(I32)[32 * q : 32 * q + ROWS, :], staged[:, q, :])
+
+        def load_plane(queue, plane, src):
+            for q in range(QUADS):
+                queue.dma_start(
+                    plane.bitcast(I32)[32 * q : 32 * q + ROWS, :], src[0, ROWS * q : ROWS * (q + 1), :].bitcast(I32)
+                )
+
+        def fp8_words(words):
+            return words[0].rearrange("p n t -> p (n t)")
+
+        cq_rows = cq.rearrange("(p t) c -> p t c", t=PACK)
+        cq_sb = [sbuf("cq%d" % t, [P, T], F32) for t in range(PACK)]
+
+        xo_plane = sbuf("xo_plane", [P, Z], U8)
+        nc.vector.memset(xo_plane[:].bitcast(I32), 0)
+        ww_plane = sbuf("ww_plane", [P, 2 * R], U8)
+        nc.vector.memset(ww_plane[:].bitcast(I32), 0)
+        late_planes = sbuf("late_planes", [P, 2 * N + O], U8)
+        nc.vector.memset(late_planes[:].bitcast(I32), 0)
+        board = [sbuf("board%d" % t, [P, C], F32) for t in range(PACK)]
+        for t in range(PACK):
+            nc.vector.memset(board[t][:], 0.0)
+        page = [sbuf("page%d" % h, [P, E], F32) for h in range(N // P)]
+        for h in range(N // P):
+            nc.vector.memset(page[h][:], 0.0)
+
+        ww_staged = sbuf("ww_staged", [ROWS, QUADS, 2 * R // 4], I32)
+        list1 = load_list("list1", offs)
+        stage_scales(ww_staged[:, :, 0 : R // 4], w_scales)
+        nc.sync.dma_start(cq_sb[0][:], cq_rows[:, 0, :])
+        stage_scales(ww_staged[:, :, R // 4 :], w2_scales)
+        list2 = load_list("list2", offs2)
+        gs_sb = load_by_slot(nc.scalar, "gs_sb", gs)
+        nc.sync.dma_start(cq_sb[1][:], cq_rows[:, 1, :])
+        load_plane(nc.gpsimd, xo_plane[:], xo_scales)
+        nc.sync.dma_start(cq_sb[2][:], cq_rows[:, 2, :])
+        list5 = load_list("list5", offs5)
+        list4 = load_list("list4", offs4)
+        nc.sync.dma_start(cq_sb[3][:], cq_rows[:, 3, :])
+        w_raw = load_words("w_raw", w_words[0], R, U16)
+        w2_raw = load_words("w2_raw", fp8_words(w2_words), R, U32)
+        xo_sb = load_words("xo_sb", xo_words[0], Z, U16)
+        list3 = load_list("list3", offs3)
+        list6 = load_list("list6", offs6)
+        sb_sb = load_by_slot(nc.gpsimd, "sb_sb", sb)
+        sg_sb = load_by_slot(nc.gpsimd, "sg_sb", sg)
+        bg_sb = load_by_slot(nc.gpsimd, "bg_sb", bg)
+        sa_sb = load_by_slot(nc.gpsimd, "sa_sb", sa)
+        ws_sb = load_words("ws_sb", fp8_words(ws_words), N, U32)
+        sx_sb = load_words("sx_sb", sx_words[0], O, U16)
+        wb_sb = load_words("wb_sb", fp8_words(wb_words), N, U32)
+        list7 = load_list("list7", offs7)
+        ws_plane = late_planes[:, 0:N]
+        wb_plane = late_planes[:, N : 2 * N]
+        sx_plane = late_planes[:, 2 * N :]
+        load_plane(nc.sync, ws_plane, ws_scales)
+        load_plane(nc.sync, sx_plane, sx_scales)
+        load_plane(nc.sync, wb_plane, wb_scales)
+
+        spread_scales(ww_plane, ww_staged)
+        w_dealt_plane = sbuf("w_dealt_plane", [P, PACK, P], U8)
+        nc.vector.tensor_copy(w_dealt_plane[:], ww_plane[:, 0:R].rearrange("p (m t) -> p t m", t=PACK))
+        w2_dealt_plane = sbuf("w2_dealt_plane", [P, PACK, P], U8)
+        nc.vector.tensor_copy(w2_dealt_plane[:], ww_plane[:, R:].rearrange("p (m t) -> p t m", t=PACK))
+        xo_picked_plane = sbuf("xo_picked_plane", [P, J], U8)
+        nc.vector.tensor_copy(xo_picked_plane[:], xo_plane[:].indirect(list2[:]))
+
+        x1_planes = sbuf("x1_planes", [P, PACK, J], BF16)
+        for t in range(PACK):
+            nc.scalar.activation(x1_planes[:, t, :], cq_sb[t][:].indirect(list1[:]), ACT.Copy, scale=gs_sb[:, t : t + 1])
+        w_dealt = sbuf("w_dealt", [P, PACK, P], U16)
+        nc.scalar.copy(w_dealt[:], w_raw[:].rearrange("p (m t) -> p t m", t=PACK))
+        w2_dealt = sbuf("w2_dealt", [P, PACK, P], U32)
+        nc.scalar.copy(w2_dealt[:], w2_raw[:].rearrange("p (m t) -> p t m", t=PACK))
+        x1_words = sbuf("x1_words", [P, J, PACK], BF16)
+        nc.vector.tensor_copy(x1_words[:], x1_planes[:].rearrange("p t j -> p j t"))
+        x1_codes = sbuf("x1_codes", [P, J], U32)
+        x1_plane = sbuf("x1_plane", [P, J], U8)
+        nc.vector.quantize_mx(x1_codes[:].bitcast(E4M3), x1_plane[:], x1_words[:].rearrange("p j t -> p (j t)"))
+        xo_picked = sbuf("xo_picked", [P, J], U16)
+        nc.vector.tensor_copy(xo_picked[:], xo_sb[:].indirect(list2[:]))
+
+        a_sb = []
+        for t in range(PACK):
+            a_ps = psum.tile([P, J], F32, name="a_ps%d" % t, tag="first%d" % t)
+            nc.tensor.matmul_mx(
+                a_ps[:], lhsT=w_dealt[:, t, :].bitcast(E2M1), lhsT_scale=w_dealt_plane[:, t, :],
+                rhs=x1_codes[:].bitcast(E4M3), rhs_scale=x1_plane[:], start=True, stop=True,
+            )
+            a_t = sbuf("a_sb%d" % t, [P, J], F32)
+            nc.scalar.copy(a_t[:], a_ps[:])
+            a_sb.append(a_t)
+
+        for t in range(PACK):
+            nc.vector.tensor_copy(board[t][:].indirect(list3[:]), a_sb[t][:])
+
+        b_sb = []
+        for t in range(PACK):
+            b_ps = psum.tile([P, J], F32, name="b_ps%d" % t, tag="second%d" % t)
+            nc.tensor.matmul_mx(
+                b_ps[:], lhsT=w2_dealt[:, t, :].bitcast(E5M2), lhsT_scale=w2_dealt_plane[:, t, :],
+                rhs=xo_picked[:].bitcast(E2M1), rhs_scale=xo_picked_plane[:], start=True, stop=True,
+            )
+            b_t = sbuf("b_sb%d" % t, [P, J], F32)
+            nc.scalar.copy(b_t[:], b_ps[:])
+            b_sb.append(b_t)
+        b_term = sbuf("b_term", [P, PACK, O], F32)
+        for t in range(PACK):
+            nc.scalar.activation(b_term[:, t, :], b_sb[t][:].indirect(list6[:]), ACT.Copy, scale=sb_sb[:, t : t + 1])
+
+        p_ps = []
+        for h in range(N // P):
+            p_h = psum.tile([P, O], F32, name="p_ps%d" % h, tag="first%d" % h)
+            nc.tensor.matmul_mx(
+                p_h[:], lhsT=ws_sb[:, P * h : P * (h + 1)].bitcast(E5M2), lhsT_scale=ws_plane[:, P * h : P * (h + 1)],
+                rhs=sx_sb[:].bitcast(E2M1), rhs_scale=sx_plane, start=True, stop=False,
+            )
+            p_ps.append(p_h)
+
+        gate = sbuf("gate", [P, PACK, O], F32)
+        value = sbuf("value", [P, PACK, O], F32)
+        gated = sbuf("gated", [P, PACK, O], F32)
+        for t in range(PACK):
+            nc.scalar.activation(
+                gate[:, t, :], board[t][:].indirect(list5[:]), ACT.Sigmoid,
+                bias=bg_sb[:, t : t + 1], scale=sg_sb[:, t : t + 1],
+            )
+            nc.scalar.activation(value[:, t, :], board[t][:].indirect(list4[:]), ACT.Copy, scale=sa_sb[:, t : t + 1])
+            nc.vector.tensor_tensor(gated[:, t, :], value[:, t, :], gate[:, t, :], ALU.mult)
+
+        hid_words = sbuf("hid_words", [P, O, PACK], BF16)
+        nc.vector.tensor_tensor(
+            hid_words[:], gated[:].rearrange("p t o -> p o t"), b_term[:].rearrange("p t o -> p o t"), ALU.subtract
+        )
+        hid_codes = sbuf("hid_codes", [P, O], U32)
+        hid_plane = sbuf("hid_plane", [P, O], U8)
+        nc.vector.quantize_mx(hid_codes[:].bitcast(E4M3), hid_plane[:], hid_words[:].rearrange("p o t -> p (o t)"))
+
+        for h in range(N // P):
+            nc.tensor.matmul_mx(
+                p_ps[h][:], lhsT=wb_sb[:, P * h : P * (h + 1)].bitcast(E5M2), lhsT_scale=wb_plane[:, P * h : P * (h + 1)],
+                rhs=hid_codes[:].bitcast(E4M3), rhs_scale=hid_plane[:], start=False, stop=True,
+            )
+            p_sb = sbuf("p_sb%d" % h, [P, O], F32)
+            if h == 0:
+                nc.vector.tensor_copy(p_sb[:], p_ps[h][:])
+                nc.vector.tensor_copy(page[h][:].indirect(list7[:]), p_sb[:])
+                nc.sync.dma_start(out[P * h : P * (h + 1), :], page[h][:])
+            else:
+                nc.scalar.copy(p_sb[:], p_ps[h][:])
+                nc.scalar.activation(page[h][:].indirect(list7[:]), p_sb[:], ACT.Copy)
+                nc.scalar.dma_start(out[P * h : P * (h + 1), :], page[h][:])

@@ -58,9 +58,9 @@ def tile_list_gatedreadless_codednote_further_scattered_kernel(
             for q in range(QUADS):
                 nc.vector.tensor_copy(plane[:].bitcast(I32)[32 * q : 32 * q + ROWS, :], staged[:, q, :])
 
-        def load_plane(queue, plane, src):
+        def load_plane(plane, src):
             for q in range(QUADS):
-                queue.dma_start(
+                nc.sync.dma_start(
                     plane.bitcast(I32)[32 * q : 32 * q + ROWS, :], src[0, ROWS * q : ROWS * (q + 1), :].bitcast(I32)
                 )
 
@@ -70,20 +70,21 @@ def tile_list_gatedreadless_codednote_further_scattered_kernel(
         cq_rows = cq.rearrange("(p t) c -> p t c", t=PACK)
         cq_sb = [sbuf("cq%d" % t, [P, T], F32) for t in range(PACK)]
 
-        xo_plane = sbuf("xo_plane", [P, Z], U8)
-        nc.vector.memset(xo_plane[:].bitcast(I32), 0)
+        warm_in = sbuf("warm_in", [P, 1], F32)
+        nc.vector.memset(warm_in[:], 0.0)
+
         ww_plane = sbuf("ww_plane", [P, 2 * R], U8)
         nc.vector.memset(ww_plane[:].bitcast(I32), 0)
+        xo_plane = sbuf("xo_plane", [P, Z], U8)
+        nc.vector.memset(xo_plane[:].bitcast(I32), 0)
         late_planes = sbuf("late_planes", [P, 2 * N + O], U8)
         nc.vector.memset(late_planes[:].bitcast(I32), 0)
         board = [sbuf("board%d" % t, [P, C], F32) for t in range(PACK)]
         for t in range(PACK):
             nc.vector.memset(board[t][:], 0.0)
-        page = [sbuf("page%d" % h, [P, E], F32) for h in range(N // P)]
-        for h in range(N // P):
-            nc.vector.memset(page[h][:], 0.0)
 
         ww_staged = sbuf("ww_staged", [ROWS, QUADS, 2 * R // 4], I32)
+        xo_staged = sbuf("xo_staged", [ROWS, QUADS, Z // 4], I32)
         list1 = load_list("list1", offs)
         stage_scales(ww_staged[:, :, 0 : R // 4], w_scales)
         nc.sync.dma_start(cq_sb[0][:], cq_rows[:, 0, :])
@@ -91,16 +92,19 @@ def tile_list_gatedreadless_codednote_further_scattered_kernel(
         list2 = load_list("list2", offs2)
         gs_sb = load_by_slot(nc.scalar, "gs_sb", gs)
         nc.sync.dma_start(cq_sb[1][:], cq_rows[:, 1, :])
-        load_plane(nc.gpsimd, xo_plane[:], xo_scales)
+        stage_scales(xo_staged[:], xo_scales)
         nc.sync.dma_start(cq_sb[2][:], cq_rows[:, 2, :])
-        list5 = load_list("list5", offs5)
-        list4 = load_list("list4", offs4)
         nc.sync.dma_start(cq_sb[3][:], cq_rows[:, 3, :])
         w_raw = load_words("w_raw", w_words[0], R, U16)
         w2_raw = load_words("w2_raw", fp8_words(w2_words), R, U32)
         xo_sb = load_words("xo_sb", xo_words[0], Z, U16)
         list3 = load_list("list3", offs3)
+        list5 = load_list("list5", offs5)
+        list4 = load_list("list4", offs4)
         list6 = load_list("list6", offs6)
+        page = [sbuf("page%d" % h, [P, E], F32) for h in range(N // P)]
+        for h in range(N // P):
+            nc.gpsimd.memset(page[h][:], 0.0)
         sb_sb = load_by_slot(nc.gpsimd, "sb_sb", sb)
         sg_sb = load_by_slot(nc.gpsimd, "sg_sb", sg)
         bg_sb = load_by_slot(nc.gpsimd, "bg_sb", bg)
@@ -112,13 +116,17 @@ def tile_list_gatedreadless_codednote_further_scattered_kernel(
         ws_plane = late_planes[:, 0:N]
         wb_plane = late_planes[:, N : 2 * N]
         sx_plane = late_planes[:, 2 * N :]
-        load_plane(nc.sync, ws_plane, ws_scales)
-        load_plane(nc.sync, sx_plane, sx_scales)
-        load_plane(nc.sync, wb_plane, wb_scales)
+        load_plane(ws_plane, ws_scales)
+        load_plane(sx_plane, sx_scales)
+        load_plane(wb_plane, wb_scales)
+
+        warm_out = sbuf("warm_out", [P, 1], F32)
+        nc.scalar.activation(warm_out[:], warm_in[:], ACT.Sigmoid, bias=warm_in[:])
 
         spread_scales(ww_plane, ww_staged)
         w_dealt_plane = sbuf("w_dealt_plane", [P, PACK, P], U8)
         nc.vector.tensor_copy(w_dealt_plane[:], ww_plane[:, 0:R].rearrange("p (m t) -> p t m", t=PACK))
+        spread_scales(xo_plane, xo_staged)
         w2_dealt_plane = sbuf("w2_dealt_plane", [P, PACK, P], U8)
         nc.vector.tensor_copy(w2_dealt_plane[:], ww_plane[:, R:].rearrange("p (m t) -> p t m", t=PACK))
         xo_picked_plane = sbuf("xo_picked_plane", [P, J], U8)
@@ -128,11 +136,12 @@ def tile_list_gatedreadless_codednote_further_scattered_kernel(
         for t in range(PACK):
             nc.scalar.activation(x1_planes[:, t, :], cq_sb[t][:].indirect(list1[:]), ACT.Copy, scale=gs_sb[:, t : t + 1])
         w_dealt = sbuf("w_dealt", [P, PACK, P], U16)
-        nc.scalar.copy(w_dealt[:], w_raw[:].rearrange("p (m t) -> p t m", t=PACK))
+        nc.scalar.copy(w_dealt[:].rearrange("p t m -> p m t"), w_raw[:].rearrange("p (m t) -> p m t", t=PACK))
         w2_dealt = sbuf("w2_dealt", [P, PACK, P], U32)
-        nc.scalar.copy(w2_dealt[:], w2_raw[:].rearrange("p (m t) -> p t m", t=PACK))
+        nc.scalar.copy(w2_dealt[:].rearrange("p t m -> p m t"), w2_raw[:].rearrange("p (m t) -> p m t", t=PACK))
         x1_words = sbuf("x1_words", [P, J, PACK], BF16)
-        nc.vector.tensor_copy(x1_words[:], x1_planes[:].rearrange("p t j -> p j t"))
+        for u in range(0, PACK, 2):
+            nc.vector.tensor_copy(x1_words[:, :, u : u + 2], x1_planes[:, u : u + 2, :].rearrange("p t j -> p j t"))
         x1_codes = sbuf("x1_codes", [P, J], U32)
         x1_plane = sbuf("x1_plane", [P, J], U8)
         nc.vector.quantize_mx(x1_codes[:].bitcast(E4M3), x1_plane[:], x1_words[:].rearrange("p j t -> p (j t)"))
@@ -150,8 +159,10 @@ def tile_list_gatedreadless_codednote_further_scattered_kernel(
             nc.scalar.copy(a_t[:], a_ps[:])
             a_sb.append(a_t)
 
-        for t in range(PACK):
+        nc.scalar.activation(board[3][:].indirect(list3[:, 0:4]), a_sb[3][:, 0:64], ACT.Copy)
+        for t in range(PACK - 1):
             nc.vector.tensor_copy(board[t][:].indirect(list3[:]), a_sb[t][:])
+        nc.vector.tensor_copy(board[3][:].indirect(list3[:, 4:]), a_sb[3][:, 64:])
 
         b_sb = []
         for t in range(PACK):
@@ -189,7 +200,10 @@ def tile_list_gatedreadless_codednote_further_scattered_kernel(
 
         hid_words = sbuf("hid_words", [P, O, PACK], BF16)
         nc.vector.tensor_tensor(
-            hid_words[:], gated[:].rearrange("p t o -> p o t"), b_term[:].rearrange("p t o -> p o t"), ALU.subtract
+            hid_words[:].rearrange("p (c i) t -> p c t i", i=4),
+            gated[:].rearrange("p t (c i) -> p c t i", i=4),
+            b_term[:].rearrange("p t (c i) -> p c t i", i=4),
+            ALU.subtract,
         )
         hid_codes = sbuf("hid_codes", [P, O], U32)
         hid_plane = sbuf("hid_plane", [P, O], U8)

@@ -73,18 +73,21 @@ def tile_list_gatedreadless_codednote_further_scattered_kernel(
         warm_in = sbuf("warm_in", [P, 1], F32)
         nc.vector.memset(warm_in[:], 0.0)
 
+        xo_staged = sbuf("xo_staged", [P, QUADS, Z // 4], I32)
+        nc.vector.memset(xo_staged[64:96, :, :], 0)
         ww_plane = sbuf("ww_plane", [P, 2 * R], U8)
         nc.vector.memset(ww_plane[:].bitcast(I32), 0)
         xo_plane = sbuf("xo_plane", [P, Z], U8)
-        nc.vector.memset(xo_plane[:].bitcast(I32), 0)
         late_planes = sbuf("late_planes", [P, 2 * N + O], U8)
         nc.vector.memset(late_planes[:].bitcast(I32), 0)
         board = [sbuf("board%d" % t, [P, C], F32) for t in range(PACK)]
         for t in range(PACK):
             nc.vector.memset(board[t][:], 0.0)
+        page = [sbuf("page%d" % h, [P, E], F32) for h in range(N // P)]
+        for h in range(N // P):
+            nc.vector.memset(page[h][:], 0.0)
 
         ww_staged = sbuf("ww_staged", [ROWS, QUADS, 2 * R // 4], I32)
-        xo_staged = sbuf("xo_staged", [ROWS, QUADS, Z // 4], I32)
         list1 = load_list("list1", offs)
         stage_scales(ww_staged[:, :, 0 : R // 4], w_scales)
         nc.sync.dma_start(cq_sb[0][:], cq_rows[:, 0, :])
@@ -92,23 +95,20 @@ def tile_list_gatedreadless_codednote_further_scattered_kernel(
         list2 = load_list("list2", offs2)
         gs_sb = load_by_slot(nc.scalar, "gs_sb", gs)
         nc.sync.dma_start(cq_sb[1][:], cq_rows[:, 1, :])
-        stage_scales(xo_staged[:], xo_scales)
+        stage_scales(xo_staged[64 : 64 + ROWS, :, :], xo_scales)
         nc.sync.dma_start(cq_sb[2][:], cq_rows[:, 2, :])
         nc.sync.dma_start(cq_sb[3][:], cq_rows[:, 3, :])
         w_raw = load_words("w_raw", w_words[0], R, U16)
         w2_raw = load_words("w2_raw", fp8_words(w2_words), R, U32)
         xo_sb = load_words("xo_sb", xo_words[0], Z, U16)
-        list3 = load_list("list3", offs3)
-        list5 = load_list("list5", offs5)
-        list4 = load_list("list4", offs4)
         list6 = load_list("list6", offs6)
-        page = [sbuf("page%d" % h, [P, E], F32) for h in range(N // P)]
-        for h in range(N // P):
-            nc.gpsimd.memset(page[h][:], 0.0)
-        sb_sb = load_by_slot(nc.gpsimd, "sb_sb", sb)
-        sg_sb = load_by_slot(nc.gpsimd, "sg_sb", sg)
-        bg_sb = load_by_slot(nc.gpsimd, "bg_sb", bg)
-        sa_sb = load_by_slot(nc.gpsimd, "sa_sb", sa)
+        sb_sb = load_by_slot(nc.sync, "sb_sb", sb)
+        list5 = load_list("list5", offs5)
+        sg_sb = load_by_slot(nc.sync, "sg_sb", sg)
+        bg_sb = load_by_slot(nc.sync, "bg_sb", bg)
+        list4 = load_list("list4", offs4)
+        list3 = load_list("list3", offs3)
+        sa_sb = load_by_slot(nc.sync, "sa_sb", sa)
         ws_sb = load_words("ws_sb", fp8_words(ws_words), N, U32)
         sx_sb = load_words("sx_sb", sx_words[0], O, U16)
         wb_sb = load_words("wb_sb", fp8_words(wb_words), N, U32)
@@ -126,7 +126,8 @@ def tile_list_gatedreadless_codednote_further_scattered_kernel(
         spread_scales(ww_plane, ww_staged)
         w_dealt_plane = sbuf("w_dealt_plane", [P, PACK, P], U8)
         nc.vector.tensor_copy(w_dealt_plane[:], ww_plane[:, 0:R].rearrange("p (m t) -> p t m", t=PACK))
-        spread_scales(xo_plane, xo_staged)
+        for q in range(QUADS):
+            nc.vector.tensor_copy(xo_plane[:].bitcast(I32)[32 * q : 32 * (q + 1), :], xo_staged[64:96, q, :])
         w2_dealt_plane = sbuf("w2_dealt_plane", [P, PACK, P], U8)
         nc.vector.tensor_copy(w2_dealt_plane[:], ww_plane[:, R:].rearrange("p (m t) -> p t m", t=PACK))
         xo_picked_plane = sbuf("xo_picked_plane", [P, J], U8)

@@ -18,9 +18,15 @@ ACT = mybir.ActivationFunctionType
 ALU = mybir.AluOpType
 
 P = 128
-PACK = 4
+SLOTS = 4
 QUADS = 4
-ROWS = 4
+QUAD = P // QUADS
+LIVE = 4
+WORD = 4
+PER_COLUMN = 16
+LINE = 4
+XO_STAGE = 64
+SCALAR_SHARE = 64
 
 
 def tile_list_gatedreadless_codednote_further_scattered_kernel(
@@ -33,8 +39,8 @@ def tile_list_gatedreadless_codednote_further_scattered_kernel(
         keep = ctx.enter_context(tc.tile_pool(name="keep", bufs=1))
         psum = ctx.enter_context(tc.psum_pool(name="psum", bufs=1))
 
-        def sbuf(name, shape, dtype):
-            return keep.tile(shape, dtype, name=name, align_bytes=64)
+        def sbuf(name, shape, dtype, tag=""):
+            return keep.tile(shape, dtype, name=name, tag=tag, align_bytes=64)
 
         def load_list(name, src):
             dst = sbuf(name, list(src.shape), U16)
@@ -42,8 +48,8 @@ def tile_list_gatedreadless_codednote_further_scattered_kernel(
             return dst
 
         def load_by_slot(queue, name, src):
-            dst = sbuf(name, [P, PACK], F32)
-            queue.dma_start(dst[:], src.rearrange("(p t) o -> p (t o)", t=PACK))
+            dst = sbuf(name, [P, SLOTS], F32)
+            queue.dma_start(dst[:], src.rearrange("(p t) o -> p (t o)", t=SLOTS))
             return dst
 
         def load_words(name, src, columns, dtype):
@@ -52,50 +58,45 @@ def tile_list_gatedreadless_codednote_further_scattered_kernel(
             return dst
 
         def stage_scales(dst, src):
-            nc.scalar.dma_start(dst, src[0].rearrange("(q r) n -> r q n", r=ROWS).bitcast(I32))
-
-        def spread_scales(plane, staged):
-            for q in range(QUADS):
-                nc.vector.tensor_copy(plane[:].bitcast(I32)[32 * q : 32 * q + ROWS, :], staged[:, q, :])
+            nc.scalar.dma_start(dst, src[0].rearrange("(q i) n -> i q n", i=LIVE).bitcast(I32))
 
         def load_plane(plane, src):
             for q in range(QUADS):
                 nc.sync.dma_start(
-                    plane.bitcast(I32)[32 * q : 32 * q + ROWS, :], src[0, ROWS * q : ROWS * (q + 1), :].bitcast(I32)
+                    plane.bitcast(I32)[QUAD * q : QUAD * q + LIVE, :], src[0, LIVE * q : LIVE * (q + 1), :].bitcast(I32)
                 )
 
         def fp8_words(words):
             return words[0].rearrange("p n t -> p (n t)")
 
-        cq_rows = cq.rearrange("(p t) c -> p t c", t=PACK)
-        cq_sb = [sbuf("cq%d" % t, [P, T], F32) for t in range(PACK)]
+        cq_rows = cq.rearrange("(p t) c -> p t c", t=SLOTS)
+        cq_sb = [sbuf("cq%d" % t, [P, T], F32) for t in range(SLOTS)]
 
         warm_in = sbuf("warm_in", [P, 1], F32)
         nc.vector.memset(warm_in[:], 0.0)
 
-        xo_staged = sbuf("xo_staged", [P, QUADS, Z // 4], I32)
-        nc.vector.memset(xo_staged[64:96, :, :], 0)
+        xo_staged = sbuf("xo_staged", [P, QUADS, Z // WORD], I32)
+        nc.vector.memset(xo_staged[XO_STAGE : XO_STAGE + QUAD, :, :], 0)
         ww_plane = sbuf("ww_plane", [P, 2 * R], U8)
         nc.vector.memset(ww_plane[:].bitcast(I32), 0)
         xo_plane = sbuf("xo_plane", [P, Z], U8)
-        late_planes = sbuf("late_planes", [P, 2 * N + O], U8)
-        nc.vector.memset(late_planes[:].bitcast(I32), 0)
-        board = [sbuf("board%d" % t, [P, C], F32) for t in range(PACK)]
-        for t in range(PACK):
+        out_planes = sbuf("out_planes", [P, 2 * N + O], U8)
+        nc.vector.memset(out_planes[:].bitcast(I32), 0)
+        board = [sbuf("board%d" % t, [P, C], F32) for t in range(SLOTS)]
+        for t in range(SLOTS):
             nc.vector.memset(board[t][:], 0.0)
-        page = [sbuf("page%d" % h, [P, E], F32) for h in range(N // P)]
-        for h in range(N // P):
-            nc.vector.memset(page[h][:], 0.0)
+        page = [sbuf("page0", [P, E], F32)]
+        nc.vector.memset(page[0][:], 0.0)
 
-        ww_staged = sbuf("ww_staged", [ROWS, QUADS, 2 * R // 4], I32)
+        ww_staged = sbuf("ww_staged", [LIVE, QUADS, 2 * R // WORD], I32)
         list1 = load_list("list1", offs)
-        stage_scales(ww_staged[:, :, 0 : R // 4], w_scales)
+        stage_scales(ww_staged[:, :, 0 : R // WORD], w_scales)
         nc.sync.dma_start(cq_sb[0][:], cq_rows[:, 0, :])
-        stage_scales(ww_staged[:, :, R // 4 :], w2_scales)
+        stage_scales(ww_staged[:, :, R // WORD :], w2_scales)
         list2 = load_list("list2", offs2)
         gs_sb = load_by_slot(nc.scalar, "gs_sb", gs)
         nc.sync.dma_start(cq_sb[1][:], cq_rows[:, 1, :])
-        stage_scales(xo_staged[64 : 64 + ROWS, :, :], xo_scales)
+        stage_scales(xo_staged[XO_STAGE : XO_STAGE + LIVE, :, :], xo_scales)
         nc.sync.dma_start(cq_sb[2][:], cq_rows[:, 2, :])
         nc.sync.dma_start(cq_sb[3][:], cq_rows[:, 3, :])
         w_raw = load_words("w_raw", w_words[0], R, U16)
@@ -113,9 +114,9 @@ def tile_list_gatedreadless_codednote_further_scattered_kernel(
         sx_sb = load_words("sx_sb", sx_words[0], O, U16)
         wb_sb = load_words("wb_sb", fp8_words(wb_words), N, U32)
         list7 = load_list("list7", offs7)
-        ws_plane = late_planes[:, 0:N]
-        wb_plane = late_planes[:, N : 2 * N]
-        sx_plane = late_planes[:, 2 * N :]
+        ws_plane = out_planes[:, 0:N]
+        wb_plane = out_planes[:, N : 2 * N]
+        sx_plane = out_planes[:, 2 * N :]
         load_plane(ws_plane, ws_scales)
         load_plane(sx_plane, sx_scales)
         load_plane(wb_plane, wb_scales)
@@ -123,26 +124,30 @@ def tile_list_gatedreadless_codednote_further_scattered_kernel(
         warm_out = sbuf("warm_out", [P, 1], F32)
         nc.scalar.activation(warm_out[:], warm_in[:], ACT.Sigmoid, bias=warm_in[:])
 
-        spread_scales(ww_plane, ww_staged)
-        w_dealt_plane = sbuf("w_dealt_plane", [P, PACK, P], U8)
-        nc.vector.tensor_copy(w_dealt_plane[:], ww_plane[:, 0:R].rearrange("p (m t) -> p t m", t=PACK))
         for q in range(QUADS):
-            nc.vector.tensor_copy(xo_plane[:].bitcast(I32)[32 * q : 32 * (q + 1), :], xo_staged[64:96, q, :])
-        w2_dealt_plane = sbuf("w2_dealt_plane", [P, PACK, P], U8)
-        nc.vector.tensor_copy(w2_dealt_plane[:], ww_plane[:, R:].rearrange("p (m t) -> p t m", t=PACK))
+            nc.vector.tensor_copy(ww_plane[:].bitcast(I32)[QUAD * q : QUAD * q + LIVE, :], ww_staged[:, q, :])
+        w_dealt_plane = sbuf("w_dealt_plane", [P, SLOTS, P], U8)
+        nc.vector.tensor_copy(w_dealt_plane[:], ww_plane[:, 0:R].rearrange("p (m t) -> p t m", t=SLOTS))
+        for q in range(QUADS):
+            nc.vector.tensor_copy(
+                xo_plane[:].bitcast(I32)[QUAD * q : QUAD * (q + 1), :], xo_staged[XO_STAGE : XO_STAGE + QUAD, q, :]
+            )
+        w2_dealt_plane = sbuf("w2_dealt_plane", [P, SLOTS, P], U8)
+        nc.vector.tensor_copy(w2_dealt_plane[:], ww_plane[:, R:].rearrange("p (m t) -> p t m", t=SLOTS))
         xo_picked_plane = sbuf("xo_picked_plane", [P, J], U8)
         nc.vector.tensor_copy(xo_picked_plane[:], xo_plane[:].indirect(list2[:]))
 
-        x1_planes = sbuf("x1_planes", [P, PACK, J], BF16)
-        for t in range(PACK):
-            nc.scalar.activation(x1_planes[:, t, :], cq_sb[t][:].indirect(list1[:]), ACT.Copy, scale=gs_sb[:, t : t + 1])
-        w_dealt = sbuf("w_dealt", [P, PACK, P], U16)
-        nc.scalar.copy(w_dealt[:].rearrange("p t m -> p m t"), w_raw[:].rearrange("p (m t) -> p m t", t=PACK))
-        w2_dealt = sbuf("w2_dealt", [P, PACK, P], U32)
-        nc.scalar.copy(w2_dealt[:].rearrange("p t m -> p m t"), w2_raw[:].rearrange("p (m t) -> p m t", t=PACK))
-        x1_words = sbuf("x1_words", [P, J, PACK], BF16)
-        for u in range(0, PACK, 2):
-            nc.vector.tensor_copy(x1_words[:, :, u : u + 2], x1_planes[:, u : u + 2, :].rearrange("p t j -> p j t"))
+        x1_slots = sbuf("x1_slots", [P, SLOTS, J], BF16)
+        x1_words = sbuf("x1_words", [P, J, SLOTS], BF16)
+        for t in range(SLOTS):
+            nc.scalar.activation(x1_slots[:, t, :], cq_sb[t][:].indirect(list1[:]), ACT.Copy, scale=gs_sb[:, t : t + 1])
+            if t == 1:
+                nc.scalar.copy(x1_words[:, :, 0:2], x1_slots[:, 0:2, :].rearrange("p t j -> p j t"))
+        w_dealt = sbuf("w_dealt", [P, SLOTS, P], U16)
+        nc.scalar.copy(w_dealt[:].rearrange("p t m -> p m t"), w_raw[:].rearrange("p (m t) -> p m t", t=SLOTS))
+        w2_dealt = sbuf("w2_dealt", [P, SLOTS, P], U32)
+        nc.scalar.copy(w2_dealt[:].rearrange("p t m -> p m t"), w2_raw[:].rearrange("p (m t) -> p m t", t=SLOTS))
+        nc.vector.tensor_copy(x1_words[:, :, 2:4], x1_slots[:, 2:4, :].rearrange("p t j -> p j t"))
         x1_codes = sbuf("x1_codes", [P, J], U32)
         x1_plane = sbuf("x1_plane", [P, J], U8)
         nc.vector.quantize_mx(x1_codes[:].bitcast(E4M3), x1_plane[:], x1_words[:].rearrange("p j t -> p (j t)"))
@@ -150,7 +155,7 @@ def tile_list_gatedreadless_codednote_further_scattered_kernel(
         nc.vector.tensor_copy(xo_picked[:], xo_sb[:].indirect(list2[:]))
 
         a_sb = []
-        for t in range(PACK):
+        for t in range(SLOTS):
             a_ps = psum.tile([P, J], F32, name="a_ps%d" % t, tag="first%d" % t)
             nc.tensor.matmul_mx(
                 a_ps[:], lhsT=w_dealt[:, t, :].bitcast(E2M1), lhsT_scale=w_dealt_plane[:, t, :],
@@ -160,13 +165,15 @@ def tile_list_gatedreadless_codednote_further_scattered_kernel(
             nc.scalar.copy(a_t[:], a_ps[:])
             a_sb.append(a_t)
 
-        nc.scalar.activation(board[3][:].indirect(list3[:, 0:4]), a_sb[3][:, 0:64], ACT.Copy)
-        for t in range(PACK - 1):
+        last = SLOTS - 1
+        share_columns = SCALAR_SHARE // PER_COLUMN
+        nc.scalar.activation(board[last][:].indirect(list3[:, 0:share_columns]), a_sb[last][:, 0:SCALAR_SHARE], ACT.Copy)
+        for t in range(last):
             nc.vector.tensor_copy(board[t][:].indirect(list3[:]), a_sb[t][:])
-        nc.vector.tensor_copy(board[3][:].indirect(list3[:, 4:]), a_sb[3][:, 64:])
+        nc.vector.tensor_copy(board[last][:].indirect(list3[:, share_columns:]), a_sb[last][:, SCALAR_SHARE:])
 
         b_sb = []
-        for t in range(PACK):
+        for t in range(SLOTS):
             b_ps = psum.tile([P, J], F32, name="b_ps%d" % t, tag="second%d" % t)
             nc.tensor.matmul_mx(
                 b_ps[:], lhsT=w2_dealt[:, t, :].bitcast(E5M2), lhsT_scale=w2_dealt_plane[:, t, :],
@@ -175,8 +182,8 @@ def tile_list_gatedreadless_codednote_further_scattered_kernel(
             b_t = sbuf("b_sb%d" % t, [P, J], F32)
             nc.scalar.copy(b_t[:], b_ps[:])
             b_sb.append(b_t)
-        b_term = sbuf("b_term", [P, PACK, O], F32)
-        for t in range(PACK):
+        b_term = sbuf("b_term", [P, SLOTS, O], F32)
+        for t in range(SLOTS):
             nc.scalar.activation(b_term[:, t, :], b_sb[t][:].indirect(list6[:]), ACT.Copy, scale=sb_sb[:, t : t + 1])
 
         p_ps = []
@@ -188,10 +195,10 @@ def tile_list_gatedreadless_codednote_further_scattered_kernel(
             )
             p_ps.append(p_h)
 
-        gate = sbuf("gate", [P, PACK, O], F32)
-        value = sbuf("value", [P, PACK, O], F32)
-        gated = sbuf("gated", [P, PACK, O], F32)
-        for t in range(PACK):
+        gate = sbuf("gate", [P, SLOTS, O], F32)
+        value = sbuf("value", [P, SLOTS, O], F32)
+        gated = sbuf("gated", [P, SLOTS, O], F32)
+        for t in range(SLOTS):
             nc.scalar.activation(
                 gate[:, t, :], board[t][:].indirect(list5[:]), ACT.Sigmoid,
                 bias=bg_sb[:, t : t + 1], scale=sg_sb[:, t : t + 1],
@@ -199,16 +206,18 @@ def tile_list_gatedreadless_codednote_further_scattered_kernel(
             nc.scalar.activation(value[:, t, :], board[t][:].indirect(list4[:]), ACT.Copy, scale=sa_sb[:, t : t + 1])
             nc.vector.tensor_tensor(gated[:, t, :], value[:, t, :], gate[:, t, :], ALU.mult)
 
-        hid_words = sbuf("hid_words", [P, O, PACK], BF16)
+        hid_words = sbuf("hid_words", [P, O, SLOTS], BF16, tag="hid_then_page")
         nc.vector.tensor_tensor(
-            hid_words[:].rearrange("p (c i) t -> p c t i", i=4),
-            gated[:].rearrange("p t (c i) -> p c t i", i=4),
-            b_term[:].rearrange("p t (c i) -> p c t i", i=4),
+            hid_words[:].rearrange("p (c i) t -> p c t i", i=LINE),
+            gated[:].rearrange("p t (c i) -> p c t i", i=LINE),
+            b_term[:].rearrange("p t (c i) -> p c t i", i=LINE),
             ALU.subtract,
         )
         hid_codes = sbuf("hid_codes", [P, O], U32)
         hid_plane = sbuf("hid_plane", [P, O], U8)
         nc.vector.quantize_mx(hid_codes[:].bitcast(E4M3), hid_plane[:], hid_words[:].rearrange("p o t -> p (o t)"))
+        page.append(sbuf("page1", [P, E], F32, tag="hid_then_page"))
+        nc.vector.memset(page[1][:], 0.0)
 
         for h in range(N // P):
             nc.tensor.matmul_mx(

from contextlib import ExitStack

import concourse.mybir as mybir

K, T, J, R, F, Z, C, O, N, L, E = 512, 1024, 256, 512, 512, 1024, 512, 128, 256, 512, 1024
FLOPS = 2 * (K * R * J + F * R * J + R * N * O + L * N * O)

F32 = mybir.dt.float32
BF16 = mybir.dt.bfloat16
I32 = mybir.dt.int32
U32 = mybir.dt.uint32
U16 = mybir.dt.uint16
U8 = mybir.dt.uint8
E4M3 = mybir.dt.float8_e4m3fn_x4
E5M2 = mybir.dt.float8_e5m2_x4
E2M1 = mybir.dt.float4_e2m1fn_x4
ACT = mybir.ActivationFunctionType
ALU = mybir.AluOpType

P = 128
SLOTS = 4
QUADS = 4
QUAD = P // QUADS
LIVE = 4
WORD = 4
PER_COLUMN = 16
LINE = 4
XO_STAGE = 64
SCALAR_SHARE = 64


def tile_list_gatedreadless_codednote_further_scattered_kernel(
    tc, xo_words, xo_scales, cq, gs, w_words, w_scales, w2_words, w2_scales, sa, sb, sg, bg,
    wb_words, wb_scales, sx_words, sx_scales, ws_words, ws_scales,
    offs, offs2, offs3, offs4, offs5, offs6, offs7, out,
):
    nc = tc.nc
    with ExitStack() as ctx:
        keep = ctx.enter_context(tc.tile_pool(name="keep", bufs=1))
        psum = ctx.enter_context(tc.psum_pool(name="psum", bufs=1))

        def sbuf(name, shape, dtype, tag=""):
            return keep.tile(shape, dtype, name=name, tag=tag, align_bytes=64)

        def load_list(name, src):
            dst = sbuf(name, list(src.shape), U16)
            nc.sync.dma_start(dst[:], src)
            return dst

        def load_by_slot(queue, name, src):
            dst = sbuf(name, [P, SLOTS], F32)
            queue.dma_start(dst[:], src.rearrange("(p t) o -> p (t o)", t=SLOTS))
            return dst

        def load_words(name, src, columns, dtype):
            dst = sbuf(name, [P, columns], dtype)
            nc.sync.dma_start(dst[:].bitcast(I32), src.bitcast(I32))
            return dst

        def stage_scales(dst, src):
            nc.scalar.dma_start(dst, src[0].rearrange("(q i) n -> i q n", i=LIVE).bitcast(I32))

        def load_plane(plane, src):
            for q in range(QUADS):
                nc.sync.dma_start(
                    plane.bitcast(I32)[QUAD * q : QUAD * q + LIVE, :], src[0, LIVE * q : LIVE * (q + 1), :].bitcast(I32)
                )

        def fp8_words(words):
            return words[0].rearrange("p n t -> p (n t)")

        cq_rows = cq.rearrange("(p t) c -> p t c", t=SLOTS)
        cq_sb = [sbuf("cq%d" % t, [P, T], F32) for t in range(SLOTS)]

        warm_in = sbuf("warm_in", [P, 1], F32)
        nc.vector.memset(warm_in[:], 0.0)

        xo_staged = sbuf("xo_staged", [P, QUADS, Z // WORD], I32)
        nc.vector.memset(xo_staged[XO_STAGE : XO_STAGE + QUAD, :, :], 0)
        ww_plane = sbuf("ww_plane", [P, 2 * R], U8)
        nc.vector.memset(ww_plane[:].bitcast(I32), 0)
        xo_plane = sbuf("xo_plane", [P, Z], U8)
        out_planes = sbuf("out_planes", [P, 2 * N + O], U8)
        nc.vector.memset(out_planes[:].bitcast(I32), 0)
        board = [sbuf("board%d" % t, [P, C], F32) for t in range(SLOTS)]
        for t in range(SLOTS):
            nc.vector.memset(board[t][:], 0.0)
        page = [sbuf("page0", [P, E], F32)]
        nc.vector.memset(page[0][:], 0.0)

        ww_staged = sbuf("ww_staged", [LIVE, QUADS, 2 * R // WORD], I32)
        list1 = load_list("list1", offs)
        stage_scales(ww_staged[:, :, 0 : R // WORD], w_scales)
        nc.sync.dma_start(cq_sb[0][:], cq_rows[:, 0, :])
        stage_scales(ww_staged[:, :, R // WORD :], w2_scales)
        list2 = load_list("list2", offs2)
        gs_sb = load_by_slot(nc.scalar, "gs_sb", gs)
        nc.sync.dma_start(cq_sb[1][:], cq_rows[:, 1, :])
        stage_scales(xo_staged[XO_STAGE : XO_STAGE + LIVE, :, :], xo_scales)
        nc.sync.dma_start(cq_sb[2][:], cq_rows[:, 2, :])
        nc.sync.dma_start(cq_sb[3][:], cq_rows[:, 3, :])
        w_raw = load_words("w_raw", w_words[0], R, U16)
        w2_raw = load_words("w2_raw", fp8_words(w2_words), R, U32)
        xo_sb = load_words("xo_sb", xo_words[0], Z, U16)
        list6 = load_list("list6", offs6)
        sb_sb = load_by_slot(nc.sync, "sb_sb", sb)
        list5 = load_list("list5", offs5)
        sg_sb = load_by_slot(nc.sync, "sg_sb", sg)
        bg_sb = load_by_slot(nc.sync, "bg_sb", bg)
        list4 = load_list("list4", offs4)
        list3 = load_list("list3", offs3)
        sa_sb = load_by_slot(nc.sync, "sa_sb", sa)
        ws_sb = load_words("ws_sb", fp8_words(ws_words), N, U32)
        sx_sb = load_words("sx_sb", sx_words[0], O, U16)
        wb_sb = load_words("wb_sb", fp8_words(wb_words), N, U32)
        list7 = load_list("list7", offs7)
        ws_plane = out_planes[:, 0:N]
        wb_plane = out_planes[:, N : 2 * N]
        sx_plane = out_planes[:, 2 * N :]
        load_plane(ws_plane, ws_scales)
        load_plane(sx_plane, sx_scales)
        load_plane(wb_plane, wb_scales)

        warm_out = sbuf("warm_out", [P, 1], F32)
        nc.scalar.activation(warm_out[:], warm_in[:], ACT.Sigmoid, bias=warm_in[:])

        for q in range(QUADS):
            nc.vector.tensor_copy(ww_plane[:].bitcast(I32)[QUAD * q : QUAD * q + LIVE, :], ww_staged[:, q, :])
        w_dealt_plane = sbuf("w_dealt_plane", [P, SLOTS, P], U8)
        nc.vector.tensor_copy(w_dealt_plane[:], ww_plane[:, 0:R].rearrange("p (m t) -> p t m", t=SLOTS))
        for q in range(QUADS):
            nc.vector.tensor_copy(
                xo_plane[:].bitcast(I32)[QUAD * q : QUAD * (q + 1), :], xo_staged[XO_STAGE : XO_STAGE + QUAD, q, :]
            )
        w2_dealt_plane = sbuf("w2_dealt_plane", [P, SLOTS, P], U8)
        nc.vector.tensor_copy(w2_dealt_plane[:], ww_plane[:, R:].rearrange("p (m t) -> p t m", t=SLOTS))
        xo_picked_plane = sbuf("xo_picked_plane", [P, J], U8)
        nc.vector.tensor_copy(xo_picked_plane[:], xo_plane[:].indirect(list2[:]))

        x1_slots = sbuf("x1_slots", [P, SLOTS, J], BF16)
        x1_words = sbuf("x1_words", [P, J, SLOTS], BF16)
        for t in range(SLOTS):
            nc.scalar.activation(x1_slots[:, t, :], cq_sb[t][:].indirect(list1[:]), ACT.Copy, scale=gs_sb[:, t : t + 1])
            if t == 1:
                nc.scalar.copy(x1_words[:, :, 0:2], x1_slots[:, 0:2, :].rearrange("p t j -> p j t"))
        w_dealt = sbuf("w_dealt", [P, SLOTS, P], U16)
        nc.scalar.copy(w_dealt[:].rearrange("p t m -> p m t"), w_raw[:].rearrange("p (m t) -> p m t", t=SLOTS))
        w2_dealt = sbuf("w2_dealt", [P, SLOTS, P], U32)
        nc.scalar.copy(w2_dealt[:].rearrange("p t m -> p m t"), w2_raw[:].rearrange("p (m t) -> p m t", t=SLOTS))
        nc.vector.tensor_copy(x1_words[:, :, 2:4], x1_slots[:, 2:4, :].rearrange("p t j -> p j t"))
        x1_codes = sbuf("x1_codes", [P, J], U32)
        x1_plane = sbuf("x1_plane", [P, J], U8)
        nc.vector.quantize_mx(x1_codes[:].bitcast(E4M3), x1_plane[:], x1_words[:].rearrange("p j t -> p (j t)"))
        xo_picked = sbuf("xo_picked", [P, J], U16)
        nc.vector.tensor_copy(xo_picked[:], xo_sb[:].indirect(list2[:]))

        a_sb = []
        for t in range(SLOTS):
            a_ps = psum.tile([P, J], F32, name="a_ps%d" % t, tag="first%d" % t)
            nc.tensor.matmul_mx(
                a_ps[:], lhsT=w_dealt[:, t, :].bitcast(E2M1), lhsT_scale=w_dealt_plane[:, t, :],
                rhs=x1_codes[:].bitcast(E4M3), rhs_scale=x1_plane[:], start=True, stop=True,
            )
            a_t = sbuf("a_sb%d" % t, [P, J], F32)
            nc.scalar.copy(a_t[:], a_ps[:])
            a_sb.append(a_t)

        last = SLOTS - 1
        share_columns = SCALAR_SHARE // PER_COLUMN
        nc.scalar.activation(board[last][:].indirect(list3[:, 0:share_columns]), a_sb[last][:, 0:SCALAR_SHARE], ACT.Copy)
        for t in range(last):
            nc.vector.tensor_copy(board[t][:].indirect(list3[:]), a_sb[t][:])
        nc.vector.tensor_copy(board[last][:].indirect(list3[:, share_columns:]), a_sb[last][:, SCALAR_SHARE:])

        b_sb = []
        for t in range(SLOTS):
            b_ps = psum.tile([P, J], F32, name="b_ps%d" % t, tag="second%d" % t)
            nc.tensor.matmul_mx(
                b_ps[:], lhsT=w2_dealt[:, t, :].bitcast(E5M2), lhsT_scale=w2_dealt_plane[:, t, :],
                rhs=xo_picked[:].bitcast(E2M1), rhs_scale=xo_picked_plane[:], start=True, stop=True,
            )
            b_t = sbuf("b_sb%d" % t, [P, J], F32)
            nc.scalar.copy(b_t[:], b_ps[:])
            b_sb.append(b_t)
        b_term = sbuf("b_term", [P, SLOTS, O], F32)
        for t in range(SLOTS):
            nc.scalar.activation(b_term[:, t, :], b_sb[t][:].indirect(list6[:]), ACT.Copy, scale=sb_sb[:, t : t + 1])

        p_ps = []
        for h in range(N // P):
            p_h = psum.tile([P, O], F32, name="p_ps%d" % h, tag="first%d" % h)
            nc.tensor.matmul_mx(
                p_h[:], lhsT=ws_sb[:, P * h : P * (h + 1)].bitcast(E5M2), lhsT_scale=ws_plane[:, P * h : P * (h + 1)],
                rhs=sx_sb[:].bitcast(E2M1), rhs_scale=sx_plane, start=True, stop=False,
            )
            p_ps.append(p_h)

        gate = sbuf("gate", [P, SLOTS, O], F32)
        value = sbuf("value", [P, SLOTS, O], F32)
        gated = sbuf("gated", [P, SLOTS, O], F32)
        for t in range(SLOTS):
            nc.scalar.activation(
                gate[:, t, :], board[t][:].indirect(list5[:]), ACT.Sigmoid,
                bias=bg_sb[:, t : t + 1], scale=sg_sb[:, t : t + 1],
            )
            nc.scalar.activation(value[:, t, :], board[t][:].indirect(list4[:]), ACT.Copy, scale=sa_sb[:, t : t + 1])
            nc.vector.tensor_tensor(gated[:, t, :], value[:, t, :], gate[:, t, :], ALU.mult)

        hid_words = sbuf("hid_words", [P, O, SLOTS], BF16, tag="hid_then_page")
        nc.vector.tensor_tensor(
            hid_words[:].rearrange("p (c i) t -> p c t i", i=LINE),
            gated[:].rearrange("p t (c i) -> p c t i", i=LINE),
            b_term[:].rearrange("p t (c i) -> p c t i", i=LINE),
            ALU.subtract,
        )
        hid_codes = sbuf("hid_codes", [P, O], U32)
        hid_plane = sbuf("hid_plane", [P, O], U8)
        nc.vector.quantize_mx(hid_codes[:].bitcast(E4M3), hid_plane[:], hid_words[:].rearrange("p o t -> p (o t)"))
        page.append(sbuf("page1", [P, E], F32, tag="hid_then_page"))
        nc.vector.memset(page[1][:], 0.0)

        for h in range(N // P):
            nc.tensor.matmul_mx(
                p_ps[h][:], lhsT=wb_sb[:, P * h : P * (h + 1)].bitcast(E5M2), lhsT_scale=wb_plane[:, P * h : P * (h + 1)],
                rhs=hid_codes[:].bitcast(E4M3), rhs_scale=hid_plane[:], start=False, stop=True,
            )
            p_sb = sbuf("p_sb%d" % h, [P, O], F32)
            if h == 0:
                nc.vector.tensor_copy(p_sb[:], p_ps[h][:])
                nc.vector.tensor_copy(page[h][:].indirect(list7[:]), p_sb[:])
                nc.sync.dma_start(out[P * h : P * (h + 1), :], page[h][:])
            else:
                nc.scalar.copy(p_sb[:], p_ps[h][:])
                nc.scalar.activation(page[h][:].indirect(list7[:]), p_sb[:], ACT.Copy)
                nc.scalar.dma_start(out[P * h : P * (h + 1), :], page[h][:])
